import numpy as np
import ml_dtypes


def mxq(x, axis, fmt="e4m3"):
    dtype, down = {"e4m3": (ml_dtypes.float8_e4m3fn, 7), "e5m2": (ml_dtypes.float8_e5m2, 14)}[fmt]
    v = np.moveaxis(np.asarray(x, np.float32).astype(ml_dtypes.bfloat16).astype(np.float64), axis, -1)
    blocks = v.reshape(v.shape[:-1] + (-1, 32))
    amax = np.abs(blocks).max(-1, keepdims=True)
    byte = np.maximum(np.where(amax > 0, np.frexp(amax)[1] - 1 + 127, 0) - down, 1)
    scale = np.exp2(byte - 127.0)
    codes = (blocks / scale).astype(np.float32).astype(dtype).astype(np.float64)
    return np.moveaxis((codes * scale).reshape(v.shape), -1, axis)


WIDE = False


def mx_kscale(k):
    if not WIDE:
        return np.ones(k)
    levels = np.array([10, -10, 5, -5, 0])
    if k % 512:
        return np.exp2(np.random.permutation(np.resize(levels, k // 32))).repeat(32)
    a = np.empty((k // 512, 16))
    for p in range(k // 512):
        a[p, :8] = np.random.permutation(np.resize(levels, 8))
        for g in range(8):
            far = levels[np.abs(levels - a[p, g]) >= 10]
            a[p, g + 8] = far[np.random.randint(len(far))]
    return np.exp2(a.ravel()).repeat(32)


def f64(x):
    return np.asarray(x).astype(np.float64)


def striped8(idx):
    return np.asarray(idx).reshape(8, -1, 16).transpose(0, 2, 1).reshape(128, -1).astype(np.uint16)


def unstriped8(offs):
    return offs.reshape(8, 16, -1).transpose(0, 2, 1).reshape(8, -1).astype(np.int64)


def pick8(x, idx, run):
    r = np.arange(len(x))
    return x[r[:, None], idx[r % (8 * run) // run]]


E2M1 = np.array([0.0, 0.5, 1.0, 1.5, 2.0, 3.0, 4.0, 6.0, -0.0, -0.5, -1.0, -1.5, -2.0, -3.0, -4.0, -6.0])


def pack_weight(w, fmt):
    k, n = w.shape
    w = f64(np.asarray(w, np.float32).astype(ml_dtypes.bfloat16)).reshape(k // 32, 32, n)
    amax = np.abs(w).max(1)
    if fmt == "e4m3":
        byte = np.frexp(amax)[1] - 1 + 127 - 7
    else:
        mant, ex = np.frexp(amax / 6.0)
        byte = np.where(mant > 0.5, ex, ex - 1) + 127
    byte = np.clip(np.where(amax > 0, byte, 1), 1, 254)
    scaled = (w * np.exp2(127.0 - byte)[:, None, :]).reshape(k, n).astype(np.float32)
    by_word = np.ascontiguousarray(scaled.reshape(k // 512, 128, 4, n).transpose(0, 1, 3, 2))
    if fmt == "e4m3":
        words = by_word.astype(ml_dtypes.float8_e4m3fn).view(np.uint8)
    else:
        c = by_word.astype(ml_dtypes.float4_e2m1fn).view(np.uint8) & 0xF
        words = (c[..., 0::2] | (c[..., 1::2] << 4)).reshape(k // 512, 128, 2 * n)
    return np.ascontiguousarray(words), np.ascontiguousarray(byte.astype(np.uint8).reshape(k // 512, 16, n))


def unpack_weight(words, scales, fmt):
    g, _, n = scales.shape
    words = np.ascontiguousarray(words).reshape(g, 128, n, -1)
    if fmt == "e4m3":
        vals = words.view(ml_dtypes.float8_e4m3fn).astype(np.float64)
    else:
        nib = np.empty((g, 128, n, 4), np.uint8)
        nib[..., 0::2] = words & 0xF
        nib[..., 1::2] = words >> 4
        vals = E2M1[nib]
    vals = vals * np.repeat(np.exp2(scales.astype(np.float64) - 127.0), 8, axis=1)[..., None]
    return vals.transpose(0, 1, 3, 2).reshape(g * 512, n)


D, V, Q, I = 512, 2048, 128, 512


def setup_inputs():
    n = np.random.standard_normal
    idx = np.stack([np.random.permutation(V)[:I] for _ in range(8)])
    fd = mx_kscale(D)
    vocp = pack_weight(n((D, V)) / fd[:, None], "e2m1")
    return {
        "hid": (n((D, Q)) * 1.0 / np.sqrt(D) * fd[:, None]).astype(np.float32),
        "voc_words": vocp[0],
        "voc_scales": vocp[1],
        "pen": (np.random.uniform(1.5, 3.0, (Q, 1))).astype(np.float32),
        "offs": striped8(idx),
    }


def reference(hid, voc_words, voc_scales, pen, offs):
    idx = unstriped8(offs)
    vocu = unpack_weight(voc_words, voc_scales, "e2m1")
    hidq = mxq(f64(hid), 0, "e4m3")
    a = hidq.T @ vocu
    dl = np.minimum(pick8(a, idx, 16) * f64(pen), pick8(a, idx, 16) / f64(pen)) - pick8(a, idx, 16)
    df = np.zeros((Q, V))
    df[np.arange(Q)[:, None], idx[np.arange(Q) % 128 // 16]] = dl
    s = a + df
    r = s - np.max(s, axis=1, keepdims=True)
    y = r - np.log(np.sum(np.exp(r), axis=1, keepdims=True))
    return y

@@ -1,0 +1,131 @@
+from contextlib import ExitStack
+
+import concourse.mybir as mybir
+
+D, V, Q, I = 512, 2048, 128, 512
+FLOPS = 2 * D * V * Q
+
+F32 = mybir.dt.float32
+BF16 = mybir.dt.bfloat16
+I32 = mybir.dt.int32
+U32 = mybir.dt.uint32
+U16 = mybir.dt.uint16
+U8 = mybir.dt.uint8
+FP8X4 = mybir.dt.float8_e4m3fn_x4
+FP4X4 = mybir.dt.float4_e2m1fn_x4
+ALU = mybir.AluOpType
+ACT = mybir.ActivationFunctionType
+AX = mybir.AxisListType
+
+P = 128
+PACK = 4
+BANK = 512
+HALF = V // 2
+FAR_BELOW = -(2.0**100)
+
+
+def tile_attend_repeatpenalty_heads_kernel(tc, hid, voc_words, voc_scales, pen, offs, out):
+    nc = tc.nc
+    with ExitStack() as ctx:
+        keep = ctx.enter_context(tc.tile_pool(name="keep", bufs=1))
+        psum = ctx.enter_context(tc.psum_pool(name="psum", bufs=1))
+
+        offsets = keep.tile([P, I // 16], U16, name="offsets")
+        hid_raw = keep.tile([P, PACK, Q], F32, name="hid_raw")
+        voc_plane = keep.tile([P, V], U8, name="voc_plane", align_bytes=64)
+        words = [keep.tile([P, V], U8, name=f"words{u}", align_bytes=64) for u in range(2)]
+        penalty = keep.tile([P, 1], F32, name="penalty")
+        window = keep.tile([P, V], F32, name="window")
+
+        nc.vector.memset(voc_plane[:].bitcast(I32), 0)
+        nc.sync.dma_start(offsets[:], offs)
+        nc.sync.dma_start(hid_raw[:], hid.rearrange("(p j) q -> p j q", j=PACK))
+        scale_rows = voc_scales[0].bitcast(I32)
+        for quad in range(4):
+            nc.scalar.dma_start(voc_plane[32 * quad : 32 * quad + 4, :].bitcast(I32), scale_rows[4 * quad : 4 * quad + 4, :])
+        word_rows = voc_words[0].bitcast(I32)
+        for u in range(2):
+            nc.sync.dma_start(words[u][:].bitcast(I32), word_rows[:, u * (V // 4) : (u + 1) * (V // 4)])
+        nc.sync.dma_start(penalty[:], pen)
+
+        nc.vector.memset(window[:], 0.0)
+        first = I // 4
+        far_a = keep.tile([P, first], F32, name="far_a")
+        nc.vector.memset(far_a[:], FAR_BELOW)
+        nc.vector.tensor_copy(window[:].indirect(offsets[:, : first // 16]), far_a[:])
+
+        hid_bf = keep.tile([P, Q, PACK], BF16, name="hid_bf", tag="stage", align_bytes=64)
+        nc.scalar.activation(hid_bf[:], hid_raw[:].rearrange("p j q -> p q j"), ACT.Copy)
+        hid_codes = keep.tile([P, Q], U32, name="hid_codes", align_bytes=64)
+        hid_plane = keep.tile([P, Q], U8, name="hid_plane", align_bytes=64)
+        nc.vector.quantize_mx(out=hid_codes[:].bitcast(FP8X4), scales=hid_plane[:], in_=hid_bf[:].rearrange("p q j -> p (q j)"))
+
+        far_b = keep.tile([P, I - first], F32, name="far_b", tag="stage", align_bytes=64)
+        nc.vector.memset(far_b[:], FAR_BELOW)
+        nc.vector.tensor_copy(window[:].indirect(offsets[:, first // 16 :]), far_b[:])
+
+        inv = keep.tile([P, 1], F32, name="inv")
+        neg_inv = keep.tile([P, 1], F32, name="neg_inv")
+        inv_sq = keep.tile([P, 1], F32, name="inv_sq")
+        pen_sq = keep.tile([P, 1], F32, name="pen_sq")
+        nc.vector.reciprocal(inv[:], penalty[:])
+        nc.vector.tensor_scalar(pen_sq[:], penalty[:], penalty[:], None, ALU.mult)
+        nc.vector.tensor_scalar(neg_inv[:], inv[:], -1.0, None, ALU.mult)
+        nc.vector.tensor_scalar(inv_sq[:], inv[:], inv[:], None, ALU.mult)
+
+        scores = keep.tile([P, V], F32, name="scores")
+        for b in range(V // BANK):
+            bank = psum.tile([P, BANK], F32, name=f"bank{b}")
+            u, c = divmod(b, 2)
+            nc.tensor.matmul_mx(
+                out=bank[:],
+                lhsT=hid_codes[:].bitcast(FP8X4),
+                lhsT_scale=hid_plane[:],
+                rhs=words[u][:, 2 * BANK * c : 2 * BANK * (c + 1)].bitcast(FP4X4),
+                rhs_scale=voc_plane[:, BANK * b : BANK * (b + 1)],
+                start=True,
+                stop=True,
+            )
+            nc.scalar.copy(scores[:, BANK * b : BANK * (b + 1)], bank[:])
+
+        masked = keep.tile([P, V], F32, name="masked")
+        spent = keep.tile([P, V], F32, name="spent")
+        neg_top = keep.tile([P, 2], F32, name="neg_top")
+        sums = keep.tile([P, 2], F32, name="sums")
+        lo, hi = slice(0, HALF), slice(HALF, V)
+        nc.vector.tensor_tensor(masked[:, lo], scores[:, lo], window[:, lo], ALU.add)
+        nc.vector.tensor_tensor(masked[:, hi], scores[:, hi], window[:, hi], ALU.add)
+        nc.vector.tensor_reduce(neg_top[:, 0:1], masked[:, lo], AX.X, ALU.max, negate=True)
+        nc.vector.tensor_scalar(spent[:, hi], masked[:, hi], -1.0, neg_top[:, 0:1], ALU.mult, ALU.min, accum_out=neg_top[:, 1:2])
+        nc.scalar.activation(spent[:, lo], masked[:, lo], ACT.Exp, bias=neg_top[:, 0:1], accum_out=sums[:, 0:1])
+        nc.scalar.activation(spent[:, hi], masked[:, hi], ACT.Exp, bias=neg_top[:, 1:2], accum_out=sums[:, 1:2])
+
+        listed = keep.tile([P, I], F32, name="listed")
+        nc.vector.tensor_copy(listed[:], scores[:].indirect(offsets[:]))
+        start = keep.tile([P, 1], F32, name="start")
+        nc.vector.tensor_scalar(start[:], neg_top[:, 1:2], inv_sq[:], neg_top[:, 1:2], ALU.mult, ALU.min)
+        neg_div = keep.tile([P, I], F32, name="neg_div")
+        least = keep.tile([P, 1], F32, name="least")
+        nc.vector.tensor_scalar(neg_div[:], listed[:], neg_inv[:], start[:], ALU.mult, ALU.min, accum_out=least[:])
+        neg_new = keep.tile([P, I], F32, name="neg_new")
+        nc.vector.scalar_tensor_tensor(neg_new[:], neg_div[:], pen_sq[:], neg_div[:], ALU.mult, ALU.max)
+        neg_max = keep.tile([P, 1], F32, name="neg_max")
+        nc.vector.tensor_scalar(neg_max[:], least[:], pen_sq[:], least[:], ALU.mult, ALU.max)
+        nc.vector.tensor_tensor(window[:].indirect(offsets[:]), neg_new[:], listed[:], ALU.add)
+
+        listed_sum = keep.tile([P, 1], F32, name="listed_sum")
+        factor = keep.tile([P, 2], F32, name="factor")
+        part = keep.tile([P, 1], F32, name="part")
+        log_sum = keep.tile([P, 1], F32, name="log_sum")
+        shift = keep.tile([P, 1], F32, name="shift")
+        nc.scalar.activation(factor[:], neg_top[:], ACT.Exp, bias=neg_max[:], scale=-1.0)
+        nc.scalar.activation(neg_div[:], neg_new[:], ACT.Exp, bias=neg_max[:], scale=-1.0, accum_out=listed_sum[:])
+        nc.scalar.activation(part[:], sums[:, 0:1], ACT.Identity, bias=listed_sum[:], scale=factor[:, 0:1])
+        nc.scalar.activation(log_sum[:], sums[:, 1:2], ACT.Ln, bias=part[:], scale=factor[:, 1:2])
+        nc.scalar.activation(shift[:], log_sum[:], ACT.Identity, bias=neg_max[:], scale=-1.0)
+
+        for b in range(V // BANK):
+            cols = slice(BANK * b, BANK * (b + 1))
+            result = keep.tile([P, BANK], F32, name=f"result{b}")
+            nc.vector.scalar_tensor_tensor(result[:], scores[:, cols], shift[:], window[:, cols], ALU.add, ALU.subtract)
+            nc.sync.dma_start(out[:, cols], result[:])

@@ -31,7 +31,11 @@ def tile_attend_repeatpenalty_heads_kernel(tc, hid, voc_words, voc_scales, pen, 
         psum = ctx.enter_context(tc.psum_pool(name="psum", bufs=1))
 
         offsets = keep.tile([P, I // 16], U16, name="offsets")
-        hid_raw = keep.tile([P, PACK, Q], F32, name="hid_raw")
+        first = 192
+        rest = I - first
+        shared = 16
+        stage = keep.tile([P, rest - shared + D], F32, name="stage")
+        hid_raw = stage[:, rest - shared :].rearrange("p (j q) -> p j q", j=PACK)
         voc_plane = keep.tile([P, V], U8, name="voc_plane", align_bytes=64)
         words = [keep.tile([P, V], U8, name=f"words{u}", align_bytes=64) for u in range(2)]
         penalty = keep.tile([P, 1], F32, name="penalty")
@@ -39,30 +43,30 @@ def tile_attend_repeatpenalty_heads_kernel(tc, hid, voc_words, voc_scales, pen, 
 
         nc.vector.memset(voc_plane[:].bitcast(I32), 0)
         nc.sync.dma_start(offsets[:], offs)
-        nc.sync.dma_start(hid_raw[:], hid.rearrange("(p j) q -> p j q", j=PACK))
+        nc.sync.dma_start(hid_raw, hid.rearrange("(p j) q -> p j q", j=PACK))
         scale_rows = voc_scales[0].bitcast(I32)
         for quad in range(4):
-            nc.scalar.dma_start(voc_plane[32 * quad : 32 * quad + 4, :].bitcast(I32), scale_rows[4 * quad : 4 * quad + 4, :])
+            nc.sync.dma_start(voc_plane[32 * quad : 32 * quad + 4, :].bitcast(I32), scale_rows[4 * quad : 4 * quad + 4, :])
         word_rows = voc_words[0].bitcast(I32)
         for u in range(2):
             nc.sync.dma_start(words[u][:].bitcast(I32), word_rows[:, u * (V // 4) : (u + 1) * (V // 4)])
         nc.sync.dma_start(penalty[:], pen)
 
+        warm = keep.tile([P, 2], F32, name="warm")
+        nc.gpsimd.memset(warm[:, 0:1], 0.0)
+        nc.scalar.activation(warm[:, 1:2], warm[:, 0:1], ACT.Exp)
         nc.vector.memset(window[:], 0.0)
-        first = I // 4
-        far_a = keep.tile([P, first], F32, name="far_a")
-        nc.vector.memset(far_a[:], FAR_BELOW)
-        nc.vector.tensor_copy(window[:].indirect(offsets[:, : first // 16]), far_a[:])
+        nc.vector.memset(stage[:, : rest - shared], FAR_BELOW)
+        nc.vector.tensor_copy(window[:].indirect(offsets[:, : first // 16]), stage[:, :first])
 
-        hid_bf = keep.tile([P, Q, PACK], BF16, name="hid_bf", tag="stage", align_bytes=64)
-        nc.scalar.activation(hid_bf[:], hid_raw[:].rearrange("p j q -> p q j"), ACT.Copy)
+        hid_bf = keep.tile([P, Q, PACK], BF16, name="hid_bf", align_bytes=64)
+        nc.scalar.copy(hid_bf[:].rearrange("p (c i) j -> p c j i", i=4), hid_raw.rearrange("p j (c i) -> p c j i", i=4))
+        nc.scalar.copy(stage[:, rest - shared : rest], stage[:, :shared])
         hid_codes = keep.tile([P, Q], U32, name="hid_codes", align_bytes=64)
         hid_plane = keep.tile([P, Q], U8, name="hid_plane", align_bytes=64)
         nc.vector.quantize_mx(out=hid_codes[:].bitcast(FP8X4), scales=hid_plane[:], in_=hid_bf[:].rearrange("p q j -> p (q j)"))
 
-        far_b = keep.tile([P, I - first], F32, name="far_b", tag="stage", align_bytes=64)
-        nc.vector.memset(far_b[:], FAR_BELOW)
-        nc.vector.tensor_copy(window[:].indirect(offsets[:, first // 16 :]), far_b[:])
+        nc.vector.tensor_copy(window[:].indirect(offsets[:, first // 16 :]), stage[:, :rest])
 
         inv = keep.tile([P, 1], F32, name="inv")
         neg_inv = keep.tile([P, 1], F32, name="neg_inv")
@@ -74,6 +78,7 @@ def tile_attend_repeatpenalty_heads_kernel(tc, hid, voc_words, voc_scales, pen, 
         nc.vector.tensor_scalar(inv_sq[:], inv[:], inv[:], None, ALU.mult)
 
         scores = keep.tile([P, V], F32, name="scores")
+        masked = keep.tile([P, V], F32, name="masked")
         for b in range(V // BANK):
             bank = psum.tile([P, BANK], F32, name=f"bank{b}")
             u, c = divmod(b, 2)
@@ -86,46 +91,51 @@ def tile_attend_repeatpenalty_heads_kernel(tc, hid, voc_words, voc_scales, pen, 
                 start=True,
                 stop=True,
             )
-            nc.scalar.copy(scores[:, BANK * b : BANK * (b + 1)], bank[:])
+            cols = slice(BANK * b, BANK * (b + 1))
+            nc.scalar.copy(scores[:, cols], bank[:])
+            if b < 2:
+                nc.vector.tensor_tensor(masked[:, cols], bank[:], window[:, cols], ALU.add)
+            else:
+                nc.gpsimd.tensor_tensor(masked[:, cols], scores[:, cols], window[:, cols], ALU.add)
 
-        masked = keep.tile([P, V], F32, name="masked")
         spent = keep.tile([P, V], F32, name="spent")
         neg_top = keep.tile([P, 2], F32, name="neg_top")
         sums = keep.tile([P, 2], F32, name="sums")
         lo, hi = slice(0, HALF), slice(HALF, V)
-        nc.vector.tensor_tensor(masked[:, lo], scores[:, lo], window[:, lo], ALU.add)
-        nc.vector.tensor_tensor(masked[:, hi], scores[:, hi], window[:, hi], ALU.add)
         nc.vector.tensor_reduce(neg_top[:, 0:1], masked[:, lo], AX.X, ALU.max, negate=True)
+        listed = keep.tile([P, I], F32, name="listed")
+        nc.vector.tensor_copy(listed[:], scores[:].indirect(offsets[:]))
         nc.vector.tensor_scalar(spent[:, hi], masked[:, hi], -1.0, neg_top[:, 0:1], ALU.mult, ALU.min, accum_out=neg_top[:, 1:2])
         nc.scalar.activation(spent[:, lo], masked[:, lo], ACT.Exp, bias=neg_top[:, 0:1], accum_out=sums[:, 0:1])
         nc.scalar.activation(spent[:, hi], masked[:, hi], ACT.Exp, bias=neg_top[:, 1:2], accum_out=sums[:, 1:2])
 
-        listed = keep.tile([P, I], F32, name="listed")
-        nc.vector.tensor_copy(listed[:], scores[:].indirect(offsets[:]))
         start = keep.tile([P, 1], F32, name="start")
         nc.vector.tensor_scalar(start[:], neg_top[:, 1:2], inv_sq[:], neg_top[:, 1:2], ALU.mult, ALU.min)
         neg_div = keep.tile([P, I], F32, name="neg_div")
         least = keep.tile([P, 1], F32, name="least")
         nc.vector.tensor_scalar(neg_div[:], listed[:], neg_inv[:], start[:], ALU.mult, ALU.min, accum_out=least[:])
         neg_new = keep.tile([P, I], F32, name="neg_new")
-        nc.vector.scalar_tensor_tensor(neg_new[:], neg_div[:], pen_sq[:], neg_div[:], ALU.mult, ALU.max)
         neg_max = keep.tile([P, 1], F32, name="neg_max")
         nc.vector.tensor_scalar(neg_max[:], least[:], pen_sq[:], least[:], ALU.mult, ALU.max)
+        nc.vector.scalar_tensor_tensor(neg_new[:], neg_div[:], pen_sq[:], neg_div[:], ALU.mult, ALU.max)
         nc.vector.tensor_tensor(window[:].indirect(offsets[:]), neg_new[:], listed[:], ALU.add)
 
         listed_sum = keep.tile([P, 1], F32, name="listed_sum")
         factor = keep.tile([P, 2], F32, name="factor")
         part = keep.tile([P, 1], F32, name="part")
+        rest_sum = keep.tile([P, 1], F32, name="rest_sum")
         log_sum = keep.tile([P, 1], F32, name="log_sum")
         shift = keep.tile([P, 1], F32, name="shift")
         nc.scalar.activation(factor[:], neg_top[:], ACT.Exp, bias=neg_max[:], scale=-1.0)
+        nc.scalar.activation(part[:], sums[:, 0:1], ACT.Copy, scale=factor[:, 0:1])
+        nc.scalar.activation(rest_sum[:], sums[:, 1:2], ACT.Identity, bias=part[:], scale=factor[:, 1:2])
         nc.scalar.activation(neg_div[:], neg_new[:], ACT.Exp, bias=neg_max[:], scale=-1.0, accum_out=listed_sum[:])
-        nc.scalar.activation(part[:], sums[:, 0:1], ACT.Identity, bias=listed_sum[:], scale=factor[:, 0:1])
-        nc.scalar.activation(log_sum[:], sums[:, 1:2], ACT.Ln, bias=part[:], scale=factor[:, 1:2])
+        nc.scalar.activation(log_sum[:], rest_sum[:], ACT.Ln, bias=listed_sum[:])
         nc.scalar.activation(shift[:], log_sum[:], ACT.Identity, bias=neg_max[:], scale=-1.0)
 
-        for b in range(V // BANK):
-            cols = slice(BANK * b, BANK * (b + 1))
-            result = keep.tile([P, BANK], F32, name=f"result{b}")
+        edges = (0, 256, 768, 1280, 1792, V)
+        for b in range(len(edges) - 1):
+            cols = slice(edges[b], edges[b + 1])
+            result = keep.tile([P, edges[b + 1] - edges[b]], F32, name=f"result{b}")
             nc.vector.scalar_tensor_tensor(result[:], scores[:, cols], shift[:], window[:, cols], ALU.add, ALU.subtract)
             nc.sync.dma_start(out[:, cols], result[:])

@@ -21,7 +21,7 @@ P = 128
 PACK = 4
 BANK = 512
 HALF = V // 2
-FAR_BELOW = -(2.0**100)
+FAR = 2.0**100
 
 
 def tile_attend_repeatpenalty_heads_kernel(tc, hid, voc_words, voc_scales, pen, offs, out):
@@ -37,26 +37,24 @@ def tile_attend_repeatpenalty_heads_kernel(tc, hid, voc_words, voc_scales, pen, 
         stage = keep.tile([P, rest - shared + D], F32, name="stage")
         hid_raw = stage[:, rest - shared :].rearrange("p (j q) -> p j q", j=PACK)
         voc_plane = keep.tile([P, V], U8, name="voc_plane", align_bytes=64)
-        words = [keep.tile([P, V], U8, name=f"words{u}", align_bytes=64) for u in range(2)]
+        words = keep.tile([P, 2 * V], U8, name="words", align_bytes=64)
         penalty = keep.tile([P, 1], F32, name="penalty")
         window = keep.tile([P, V], F32, name="window")
 
         nc.vector.memset(voc_plane[:].bitcast(I32), 0)
         nc.sync.dma_start(offsets[:], offs)
-        nc.sync.dma_start(hid_raw, hid.rearrange("(p j) q -> p j q", j=PACK))
+        nc.sync.dma_start(penalty[:], pen)
+        nc.scalar.dma_start(hid_raw, hid.rearrange("(p j) q -> p j q", j=PACK))
+        nc.scalar.dma_start(words[:].bitcast(I32), voc_words[0].bitcast(I32))
         scale_rows = voc_scales[0].bitcast(I32)
         for quad in range(4):
             nc.sync.dma_start(voc_plane[32 * quad : 32 * quad + 4, :].bitcast(I32), scale_rows[4 * quad : 4 * quad + 4, :])
-        word_rows = voc_words[0].bitcast(I32)
-        for u in range(2):
-            nc.sync.dma_start(words[u][:].bitcast(I32), word_rows[:, u * (V // 4) : (u + 1) * (V // 4)])
-        nc.sync.dma_start(penalty[:], pen)
 
         warm = keep.tile([P, 2], F32, name="warm")
         nc.gpsimd.memset(warm[:, 0:1], 0.0)
         nc.scalar.activation(warm[:, 1:2], warm[:, 0:1], ACT.Exp)
         nc.vector.memset(window[:], 0.0)
-        nc.vector.memset(stage[:, : rest - shared], FAR_BELOW)
+        nc.vector.memset(stage[:, : rest - shared], FAR)
         nc.vector.tensor_copy(window[:].indirect(offsets[:, : first // 16]), stage[:, :first])
 
         hid_bf = keep.tile([P, Q, PACK], BF16, name="hid_bf", align_bytes=64)
@@ -68,72 +66,63 @@ def tile_attend_repeatpenalty_heads_kernel(tc, hid, voc_words, voc_scales, pen, 
 
         nc.vector.tensor_copy(window[:].indirect(offsets[:, first // 16 :]), stage[:, :rest])
 
-        inv = keep.tile([P, 1], F32, name="inv")
+        neg_pen = keep.tile([P, 1], F32, name="neg_pen")
         neg_inv = keep.tile([P, 1], F32, name="neg_inv")
-        inv_sq = keep.tile([P, 1], F32, name="inv_sq")
-        pen_sq = keep.tile([P, 1], F32, name="pen_sq")
-        nc.vector.reciprocal(inv[:], penalty[:])
-        nc.vector.tensor_scalar(pen_sq[:], penalty[:], penalty[:], None, ALU.mult)
-        nc.vector.tensor_scalar(neg_inv[:], inv[:], -1.0, None, ALU.mult)
-        nc.vector.tensor_scalar(inv_sq[:], inv[:], inv[:], None, ALU.mult)
+        nc.gpsimd.tensor_scalar(neg_pen[:], penalty[:], -1.0, 0.0, ALU.mult, ALU.add)
+        nc.vector.reciprocal(neg_inv[:], neg_pen[:])
 
         scores = keep.tile([P, V], F32, name="scores")
-        masked = keep.tile([P, V], F32, name="masked")
+        lower = keep.tile([P, HALF], F32, name="lower")
+        upper = keep.tile([P, HALF + 1], F32, name="upper")
+        fresh = keep.tile([P, I + 1], F32, name="fresh")
         for b in range(V // BANK):
             bank = psum.tile([P, BANK], F32, name=f"bank{b}")
-            u, c = divmod(b, 2)
             nc.tensor.matmul_mx(
                 out=bank[:],
                 lhsT=hid_codes[:].bitcast(FP8X4),
                 lhsT_scale=hid_plane[:],
-                rhs=words[u][:, 2 * BANK * c : 2 * BANK * (c + 1)].bitcast(FP4X4),
+                rhs=words[:, 2 * BANK * b : 2 * BANK * (b + 1)].bitcast(FP4X4),
                 rhs_scale=voc_plane[:, BANK * b : BANK * (b + 1)],
                 start=True,
                 stop=True,
             )
             cols = slice(BANK * b, BANK * (b + 1))
+            if b >= 2:
+                at = slice(BANK * (b - 2), BANK * (b - 1))
+                nc.vector.tensor_tensor(lower[:, at], window[:, cols], bank[:], ALU.subtract)
             nc.scalar.copy(scores[:, cols], bank[:])
-            if b < 2:
-                nc.vector.tensor_tensor(masked[:, cols], bank[:], window[:, cols], ALU.add)
-            else:
-                nc.gpsimd.tensor_tensor(masked[:, cols], scores[:, cols], window[:, cols], ALU.add)
+            if b == 1:
+                nc.gpsimd.tensor_tensor(upper[:, :HALF], window[:, :HALF], scores[:, :HALF], ALU.subtract)
 
-        spent = keep.tile([P, V], F32, name="spent")
-        neg_top = keep.tile([P, 2], F32, name="neg_top")
-        sums = keep.tile([P, 2], F32, name="sums")
-        lo, hi = slice(0, HALF), slice(HALF, V)
-        nc.vector.tensor_reduce(neg_top[:, 0:1], masked[:, lo], AX.X, ALU.max, negate=True)
+        lower_least, upper_least = upper[:, HALF:], fresh[:, I:]
+        lower_exp = keep.tile([P, HALF], F32, name="lower_exp")
+        upper_exp = keep.tile([P, HALF + 1], F32, name="upper_exp")
+        fresh_exp = keep.tile([P, I + 1], F32, name="fresh_exp")
         listed = keep.tile([P, I], F32, name="listed")
-        nc.vector.tensor_copy(listed[:], scores[:].indirect(offsets[:]))
-        nc.vector.tensor_scalar(spent[:, hi], masked[:, hi], -1.0, neg_top[:, 0:1], ALU.mult, ALU.min, accum_out=neg_top[:, 1:2])
-        nc.scalar.activation(spent[:, lo], masked[:, lo], ACT.Exp, bias=neg_top[:, 0:1], accum_out=sums[:, 0:1])
-        nc.scalar.activation(spent[:, hi], masked[:, hi], ACT.Exp, bias=neg_top[:, 1:2], accum_out=sums[:, 1:2])
-
-        start = keep.tile([P, 1], F32, name="start")
-        nc.vector.tensor_scalar(start[:], neg_top[:, 1:2], inv_sq[:], neg_top[:, 1:2], ALU.mult, ALU.min)
         neg_div = keep.tile([P, I], F32, name="neg_div")
-        least = keep.tile([P, 1], F32, name="least")
-        nc.vector.tensor_scalar(neg_div[:], listed[:], neg_inv[:], start[:], ALU.mult, ALU.min, accum_out=least[:])
-        neg_new = keep.tile([P, I], F32, name="neg_new")
-        neg_max = keep.tile([P, 1], F32, name="neg_max")
-        nc.vector.tensor_scalar(neg_max[:], least[:], pen_sq[:], least[:], ALU.mult, ALU.max)
-        nc.vector.scalar_tensor_tensor(neg_new[:], neg_div[:], pen_sq[:], neg_div[:], ALU.mult, ALU.max)
-        nc.vector.tensor_tensor(window[:].indirect(offsets[:]), neg_new[:], listed[:], ALU.add)
+        names = ("neg_max", "lower_sum", "lower_rest", "upper_sum", "both_sum", "both_rest", "fresh_sum", "log_sum", "shift")
+        neg_max, lower_sum, lower_rest, upper_sum, both_sum, both_rest, fresh_sum, log_sum, shift = (
+            keep.tile([P, 1], F32, name=name) for name in names
+        )
+        nc.vector.tensor_reduce(lower_least, lower[:], AX.X, ALU.min)
+        nc.vector.tensor_copy(listed[:], scores[:].indirect(offsets[:]))
+        nc.vector.tensor_reduce(upper_least, upper[:], AX.X, ALU.min)
+        nc.scalar.activation(lower_exp[:], lower[:], ACT.Exp, bias=lower_least, scale=-1.0, accum_out=lower_sum[:])
+        nc.scalar.activation(neg_div[:], listed[:], ACT.Copy, scale=neg_inv[:])
+        nc.scalar.activation(lower_rest[:], lower_sum[:], ACT.Copy, bias=-1.0)
+        nc.scalar.activation(upper_exp[:], upper[:], ACT.Exp, bias=upper_least, scale=-1.0, accum_out=upper_sum[:])
+        nc.scalar.activation(both_sum[:], lower_rest[:], ACT.Identity, bias=upper_sum[:], scale=upper_exp[:, HALF:])
+        nc.scalar.activation(both_rest[:], both_sum[:], ACT.Copy, bias=-1.0)
 
-        listed_sum = keep.tile([P, 1], F32, name="listed_sum")
-        factor = keep.tile([P, 2], F32, name="factor")
-        part = keep.tile([P, 1], F32, name="part")
-        rest_sum = keep.tile([P, 1], F32, name="rest_sum")
-        log_sum = keep.tile([P, 1], F32, name="log_sum")
-        shift = keep.tile([P, 1], F32, name="shift")
-        nc.scalar.activation(factor[:], neg_top[:], ACT.Exp, bias=neg_max[:], scale=-1.0)
-        nc.scalar.activation(part[:], sums[:, 0:1], ACT.Copy, scale=factor[:, 0:1])
-        nc.scalar.activation(rest_sum[:], sums[:, 1:2], ACT.Identity, bias=part[:], scale=factor[:, 1:2])
-        nc.scalar.activation(neg_div[:], neg_new[:], ACT.Exp, bias=neg_max[:], scale=-1.0, accum_out=listed_sum[:])
-        nc.scalar.activation(log_sum[:], rest_sum[:], ACT.Ln, bias=listed_sum[:])
+        nc.vector.scalar_tensor_tensor(fresh[:, :I], listed[:], neg_pen[:], neg_div[:], ALU.mult, ALU.max)
+        nc.vector.tensor_reduce(neg_max[:], fresh[:], AX.X, ALU.min)
+        nc.vector.tensor_tensor(window[:].indirect(offsets[:]), fresh[:, :I], listed[:], ALU.add)
+
+        nc.scalar.activation(fresh_exp[:], fresh[:], ACT.Exp, bias=neg_max[:], scale=-1.0, accum_out=fresh_sum[:])
+        nc.scalar.activation(log_sum[:], both_rest[:], ACT.Ln, bias=fresh_sum[:], scale=fresh_exp[:, I:])
         nc.scalar.activation(shift[:], log_sum[:], ACT.Identity, bias=neg_max[:], scale=-1.0)
 
-        edges = (0, 256, 768, 1280, 1792, V)
+        edges = (0, 128, 384, 896, 1408, 1792, V)
         for b in range(len(edges) - 1):
             cols = slice(edges[b], edges[b + 1])
             result = keep.tile([P, edges[b + 1] - edges[b]], F32, name=f"result{b}")

@@ -36,7 +36,7 @@ def tile_attend_repeatpenalty_heads_kernel(tc, hid, voc_words, voc_scales, pen, 
         shared = 16
         stage = keep.tile([P, rest - shared + D], F32, name="stage")
         hid_raw = stage[:, rest - shared :].rearrange("p (j q) -> p j q", j=PACK)
-        voc_plane = keep.tile([P, V], U8, name="voc_plane", align_bytes=64)
+        voc_plane = keep.tile([P, V + 4], U8, name="voc_plane", align_bytes=64)
         words = keep.tile([P, 2 * V], U8, name="words", align_bytes=64)
         penalty = keep.tile([P, 1], F32, name="penalty")
         window = keep.tile([P, V], F32, name="window")
@@ -48,13 +48,16 @@ def tile_attend_repeatpenalty_heads_kernel(tc, hid, voc_words, voc_scales, pen, 
         nc.scalar.dma_start(words[:].bitcast(I32), voc_words[0].bitcast(I32))
         scale_rows = voc_scales[0].bitcast(I32)
         for quad in range(4):
-            nc.sync.dma_start(voc_plane[32 * quad : 32 * quad + 4, :].bitcast(I32), scale_rows[4 * quad : 4 * quad + 4, :])
+            nc.sync.dma_start(voc_plane[32 * quad : 32 * quad + 4, :V].bitcast(I32), scale_rows[4 * quad : 4 * quad + 4, :])
 
-        warm = keep.tile([P, 2], F32, name="warm")
-        nc.gpsimd.memset(warm[:, 0:1], 0.0)
-        nc.scalar.activation(warm[:, 1:2], warm[:, 0:1], ACT.Exp)
-        nc.vector.memset(window[:], 0.0)
-        nc.vector.memset(stage[:, : rest - shared], FAR)
+        warm = keep.tile([P, 1], F32, name="warm")
+        nc.scalar.activation(warm[:], voc_plane[:, V:].bitcast(F32), ACT.Exp)
+        pool_share = 936
+        middle = (pool_share + V) // 2 + 1
+        nc.gpsimd.memset(stage[:, : rest - shared], FAR)
+        nc.gpsimd.memset(window[:, :pool_share], 0.0)
+        nc.vector.memset(window[:, pool_share:middle], 0.0)
+        nc.vector.memset(window[:, middle:], 0.0)
         nc.vector.tensor_copy(window[:].indirect(offsets[:, : first // 16]), stage[:, :first])
 
         hid_bf = keep.tile([P, Q, PACK], BF16, name="hid_bf", align_bytes=64)

from contextlib import ExitStack

import concourse.mybir as mybir

D, V, Q, I = 512, 2048, 128, 512
FLOPS = 2 * D * V * Q

F32 = mybir.dt.float32
BF16 = mybir.dt.bfloat16
I32 = mybir.dt.int32
U32 = mybir.dt.uint32
U16 = mybir.dt.uint16
U8 = mybir.dt.uint8
FP8X4 = mybir.dt.float8_e4m3fn_x4
FP4X4 = mybir.dt.float4_e2m1fn_x4
ALU = mybir.AluOpType
ACT = mybir.ActivationFunctionType
AX = mybir.AxisListType

P = 128
PACK = 4
BANK = 512
HALF = V // 2
FAR = 2.0**100


def tile_attend_repeatpenalty_heads_kernel(tc, hid, voc_words, voc_scales, pen, offs, out):
    nc = tc.nc
    with ExitStack() as ctx:
        keep = ctx.enter_context(tc.tile_pool(name="keep", bufs=1))
        psum = ctx.enter_context(tc.psum_pool(name="psum", bufs=1))

        offsets = keep.tile([P, I // 16], U16, name="offsets")
        first = 192
        rest = I - first
        shared = 16
        stage = keep.tile([P, rest - shared + D], F32, name="stage")
        hid_raw = stage[:, rest - shared :].rearrange("p (j q) -> p j q", j=PACK)
        voc_plane = keep.tile([P, V + 4], U8, name="voc_plane", align_bytes=64)
        words = keep.tile([P, 2 * V], U8, name="words", align_bytes=64)
        penalty = keep.tile([P, 1], F32, name="penalty")
        window = keep.tile([P, V], F32, name="window")

        nc.vector.memset(voc_plane[:].bitcast(I32), 0)
        nc.sync.dma_start(offsets[:], offs)
        nc.sync.dma_start(penalty[:], pen)
        nc.scalar.dma_start(hid_raw, hid.rearrange("(p j) q -> p j q", j=PACK))
        nc.scalar.dma_start(words[:].bitcast(I32), voc_words[0].bitcast(I32))
        scale_rows = voc_scales[0].bitcast(I32)
        for quad in range(4):
            nc.sync.dma_start(voc_plane[32 * quad : 32 * quad + 4, :V].bitcast(I32), scale_rows[4 * quad : 4 * quad + 4, :])

        warm = keep.tile([P, 1], F32, name="warm")
        nc.scalar.activation(warm[:], voc_plane[:, V:].bitcast(F32), ACT.Exp)
        pool_share = 936
        middle = (pool_share + V) // 2 + 1
        nc.gpsimd.memset(stage[:, : rest - shared], FAR)
        nc.gpsimd.memset(window[:, :pool_share], 0.0)
        nc.vector.memset(window[:, pool_share:middle], 0.0)
        nc.vector.memset(window[:, middle:], 0.0)
        nc.vector.tensor_copy(window[:].indirect(offsets[:, : first // 16]), stage[:, :first])

        hid_bf = keep.tile([P, Q, PACK], BF16, name="hid_bf", align_bytes=64)
        nc.scalar.copy(hid_bf[:].rearrange("p (c i) j -> p c j i", i=4), hid_raw.rearrange("p j (c i) -> p c j i", i=4))
        nc.scalar.copy(stage[:, rest - shared : rest], stage[:, :shared])
        hid_codes = keep.tile([P, Q], U32, name="hid_codes", align_bytes=64)
        hid_plane = keep.tile([P, Q], U8, name="hid_plane", align_bytes=64)
        nc.vector.quantize_mx(out=hid_codes[:].bitcast(FP8X4), scales=hid_plane[:], in_=hid_bf[:].rearrange("p q j -> p (q j)"))

        nc.vector.tensor_copy(window[:].indirect(offsets[:, first // 16 :]), stage[:, :rest])

        neg_pen = keep.tile([P, 1], F32, name="neg_pen")
        neg_inv = keep.tile([P, 1], F32, name="neg_inv")
        nc.gpsimd.tensor_scalar(neg_pen[:], penalty[:], -1.0, 0.0, ALU.mult, ALU.add)
        nc.vector.reciprocal(neg_inv[:], neg_pen[:])

        scores = keep.tile([P, V], F32, name="scores")
        lower = keep.tile([P, HALF], F32, name="lower")
        upper = keep.tile([P, HALF + 1], F32, name="upper")
        fresh = keep.tile([P, I + 1], F32, name="fresh")
        for b in range(V // BANK):
            bank = psum.tile([P, BANK], F32, name=f"bank{b}")
            nc.tensor.matmul_mx(
                out=bank[:],
                lhsT=hid_codes[:].bitcast(FP8X4),
                lhsT_scale=hid_plane[:],
                rhs=words[:, 2 * BANK * b : 2 * BANK * (b + 1)].bitcast(FP4X4),
                rhs_scale=voc_plane[:, BANK * b : BANK * (b + 1)],
                start=True,
                stop=True,
            )
            cols = slice(BANK * b, BANK * (b + 1))
            if b >= 2:
                at = slice(BANK * (b - 2), BANK * (b - 1))
                nc.vector.tensor_tensor(lower[:, at], window[:, cols], bank[:], ALU.subtract)
            nc.scalar.copy(scores[:, cols], bank[:])
            if b == 1:
                nc.gpsimd.tensor_tensor(upper[:, :HALF], window[:, :HALF], scores[:, :HALF], ALU.subtract)

        lower_least, upper_least = upper[:, HALF:], fresh[:, I:]
        lower_exp = keep.tile([P, HALF], F32, name="lower_exp")
        upper_exp = keep.tile([P, HALF + 1], F32, name="upper_exp")
        fresh_exp = keep.tile([P, I + 1], F32, name="fresh_exp")
        listed = keep.tile([P, I], F32, name="listed")
        neg_div = keep.tile([P, I], F32, name="neg_div")
        names = ("neg_max", "lower_sum", "lower_rest", "upper_sum", "both_sum", "both_rest", "fresh_sum", "log_sum", "shift")
        neg_max, lower_sum, lower_rest, upper_sum, both_sum, both_rest, fresh_sum, log_sum, shift = (
            keep.tile([P, 1], F32, name=name) for name in names
        )
        nc.vector.tensor_reduce(lower_least, lower[:], AX.X, ALU.min)
        nc.vector.tensor_copy(listed[:], scores[:].indirect(offsets[:]))
        nc.vector.tensor_reduce(upper_least, upper[:], AX.X, ALU.min)
        nc.scalar.activation(lower_exp[:], lower[:], ACT.Exp, bias=lower_least, scale=-1.0, accum_out=lower_sum[:])
        nc.scalar.activation(neg_div[:], listed[:], ACT.Copy, scale=neg_inv[:])
        nc.scalar.activation(lower_rest[:], lower_sum[:], ACT.Copy, bias=-1.0)
        nc.scalar.activation(upper_exp[:], upper[:], ACT.Exp, bias=upper_least, scale=-1.0, accum_out=upper_sum[:])
        nc.scalar.activation(both_sum[:], lower_rest[:], ACT.Identity, bias=upper_sum[:], scale=upper_exp[:, HALF:])
        nc.scalar.activation(both_rest[:], both_sum[:], ACT.Copy, bias=-1.0)

        nc.vector.scalar_tensor_tensor(fresh[:, :I], listed[:], neg_pen[:], neg_div[:], ALU.mult, ALU.max)
        nc.vector.tensor_reduce(neg_max[:], fresh[:], AX.X, ALU.min)
        nc.vector.tensor_tensor(window[:].indirect(offsets[:]), fresh[:, :I], listed[:], ALU.add)

        nc.scalar.activation(fresh_exp[:], fresh[:], ACT.Exp, bias=neg_max[:], scale=-1.0, accum_out=fresh_sum[:])
        nc.scalar.activation(log_sum[:], both_rest[:], ACT.Ln, bias=fresh_sum[:], scale=fresh_exp[:, I:])
        nc.scalar.activation(shift[:], log_sum[:], ACT.Identity, bias=neg_max[:], scale=-1.0)

        edges = (0, 128, 384, 896, 1408, 1792, V)
        for b in range(len(edges) - 1):
            cols = slice(edges[b], edges[b + 1])
            result = keep.tile([P, edges[b + 1] - edges[b]], F32, name=f"result{b}")
            nc.vector.scalar_tensor_tensor(result[:], scores[:, cols], shift[:], window[:, cols], ALU.add, ALU.subtract)
            nc.sync.dma_start(out[:, cols], result[:])
